import numpy as np
import ml_dtypes


def mxq(x, axis, fmt="e4m3"):
    dtype, down = {"e4m3": (ml_dtypes.float8_e4m3fn, 7), "e5m2": (ml_dtypes.float8_e5m2, 14)}[fmt]
    v = np.moveaxis(np.asarray(x, np.float32).astype(ml_dtypes.bfloat16).astype(np.float64), axis, -1)
    blocks = v.reshape(v.shape[:-1] + (-1, 32))
    amax = np.abs(blocks).max(-1, keepdims=True)
    byte = np.maximum(np.where(amax > 0, np.frexp(amax)[1] - 1 + 127, 0) - down, 1)
    scale = np.exp2(byte - 127.0)
    codes = (blocks / scale).astype(np.float32).astype(dtype).astype(np.float64)
    return np.moveaxis((codes * scale).reshape(v.shape), -1, axis)


WIDE = False


def mx_kscale(k):
    if not WIDE:
        return np.ones(k)
    levels = np.array([10, -10, 5, -5, 0])
    if k % 512:
        return np.exp2(np.random.permutation(np.resize(levels, k // 32))).repeat(32)
    a = np.empty((k // 512, 16))
    for p in range(k // 512):
        a[p, :8] = np.random.permutation(np.resize(levels, 8))
        for g in range(8):
            far = levels[np.abs(levels - a[p, g]) >= 10]
            a[p, g + 8] = far[np.random.randint(len(far))]
    return np.exp2(a.ravel()).repeat(32)


def f64(x):
    return np.asarray(x).astype(np.float64)


def striped(idx):
    return np.tile(idx.reshape(-1, 16).T, (8, 1)).astype(np.uint16)


def unstriped(offs):
    return offs[:16].T.reshape(-1).astype(np.int64)


E2M1 = np.array([0.0, 0.5, 1.0, 1.5, 2.0, 3.0, 4.0, 6.0, -0.0, -0.5, -1.0, -1.5, -2.0, -3.0, -4.0, -6.0])


def pack_weight(w, fmt):
    k, n = w.shape
    w = f64(np.asarray(w, np.float32).astype(ml_dtypes.bfloat16)).reshape(k // 32, 32, n)
    amax = np.abs(w).max(1)
    if fmt == "e4m3":
        byte = np.frexp(amax)[1] - 1 + 127 - 7
    else:
        mant, ex = np.frexp(amax / 6.0)
        byte = np.where(mant > 0.5, ex, ex - 1) + 127
    byte = np.clip(np.where(amax > 0, byte, 1), 1, 254)
    scaled = (w * np.exp2(127.0 - byte)[:, None, :]).reshape(k, n).astype(np.float32)
    by_word = np.ascontiguousarray(scaled.reshape(k // 512, 128, 4, n).transpose(0, 1, 3, 2))
    if fmt == "e4m3":
        words = by_word.astype(ml_dtypes.float8_e4m3fn).view(np.uint8)
    else:
        c = by_word.astype(ml_dtypes.float4_e2m1fn).view(np.uint8) & 0xF
        words = (c[..., 0::2] | (c[..., 1::2] << 4)).reshape(k // 512, 128, 2 * n)
    return np.ascontiguousarray(words), np.ascontiguousarray(byte.astype(np.uint8).reshape(k // 512, 16, n))


def unpack_weight(words, scales, fmt):
    g, _, n = scales.shape
    words = np.ascontiguousarray(words).reshape(g, 128, n, -1)
    if fmt == "e4m3":
        vals = words.view(ml_dtypes.float8_e4m3fn).astype(np.float64)
    else:
        nib = np.empty((g, 128, n, 4), np.uint8)
        nib[..., 0::2] = words & 0xF
        nib[..., 1::2] = words >> 4
        vals = E2M1[nib]
    vals = vals * np.repeat(np.exp2(scales.astype(np.float64) - 127.0), 8, axis=1)[..., None]
    return vals.transpose(0, 1, 3, 2).reshape(g * 512, n)


def gelu(v):
    return 0.5 * v * (1.0 + np.tanh(np.sqrt(2.0 / np.pi) * (v + 0.044715 * v**3)))


K, T, E, C, H, N = 1536, 512, 4, 128, 512, 384


def by_expert(wq, xq):
    return np.concatenate([wq[e].T @ xq[:, e * C:(e + 1) * C] for e in range(E)], axis=1)


def setup_inputs():
    n = np.random.standard_normal
    s = mx_kscale(K)[:, None]
    u = mx_kscale(H)
    w1 = [pack_weight(m, "e2m1") for m in n((E + 1, K, H)) / np.sqrt(K) / s[None] * u[None, None, :]]
    w2 = [pack_weight(m, "e2m1") for m in n((E + 1, H, N)) / np.sqrt(H) / u[None, :, None]]
    return {
        "xT": (n((K, T)) * s).astype(np.float32),
        "w1_words": np.stack([m[0] for m in w1]),
        "w1_scales": np.stack([m[1] for m in w1]),
        "w2_words": np.stack([m[0] for m in w2]),
        "w2_scales": np.stack([m[1] for m in w2]),
        "gate": np.tile(np.random.uniform(0.2, 1.0, E * C), (N, 1)).astype(np.float32),
        "offs": striped(np.random.permutation(T)[:E * C]),
    }


def reference(xT, w1_words, w1_scales, w2_words, w2_scales, gate, offs):
    idx = unstriped(offs)
    w1 = np.stack([unpack_weight(w1_words[e], w1_scales[e], "e2m1") for e in range(E + 1)])
    w2 = np.stack([unpack_weight(w2_words[e], w2_scales[e], "e2m1") for e in range(E + 1)])
    w1q, w2q = w1, w2
    xs = mxq(f64(xT), 0, "e4m3")
    hs = gelu(w1q[E].T @ xs)
    ys = w2q[E].T @ mxq(hs, 0, "e4m3")
    xq = mxq(f64(xT)[:, idx], 0, "e4m3")
    h = gelu(by_expert(w1q, xq))
    y = by_expert(w2q, mxq(h, 0, "e4m3"))
    out = ys
    out[:, idx] += f64(gate) * y
    return out

@@ -1,0 +1,244 @@
+from contextlib import ExitStack
+
+import concourse.mybir as mybir
+from concourse.masks import make_identity
+
+FLOPS = 2013265920
+
+K, T, E, C, H, N = 1536, 512, 4, 128, 512, 384
+P = 128
+SHARED = E
+PASSES = K // 512
+NB = N // P
+
+F32 = mybir.dt.float32
+BF16 = mybir.dt.bfloat16
+I32 = mybir.dt.int32
+U32 = mybir.dt.uint32
+U16 = mybir.dt.uint16
+U8 = mybir.dt.uint8
+FP8X4 = mybir.dt.float8_e4m3fn_x4
+FP4X4 = mybir.dt.float4_e2m1fn_x4
+ADD = mybir.AluOpType.add
+MULT = mybir.AluOpType.mult
+GELU = mybir.ActivationFunctionType.Gelu_apprx_tanh
+
+
+def tile_moe_shr_mlp_gelu_kernel(
+    tc, xT, w1_words, w1_scales, w2_words, w2_scales, gate, offs, out
+):
+    nc = tc.nc
+    with ExitStack() as ctx:
+        keep = ctx.enter_context(tc.tile_pool(name="keep", bufs=1))
+        work = ctx.enter_context(tc.tile_pool(name="work", bufs=2))
+        ps_l1 = ctx.enter_context(tc.psum_pool(name="ps_l1", bufs=2))
+        ps_t = ctx.enter_context(tc.psum_pool(name="ps_t", bufs=2))
+        ps_y = ctx.enter_context(tc.psum_pool(name="ps_y", bufs=1))
+
+        offsets = keep.tile([P, E * C // 16], U16, name="offsets")
+        w1_planes = keep.tile([P, (E + 1) * PASSES, H], U8, name="w1_planes", align_bytes=64)
+        w2_planes = keep.tile([P, E + 1, N], U8, name="w2_planes", align_bytes=64)
+        w2_t = keep.tile([P, E + 1, 2 * N], U8, name="w2_t", align_bytes=64)
+        w1_t = [keep.tile([P, PASSES, 2 * H], U8, name=f"w1_t{e}", align_bytes=64) for e in range(E + 1)]
+        gate_t = keep.tile([P, NB, E * C], F32, name="gate_t")
+        ident = keep.tile([P, P], F32, name="ident")
+        warm = keep.tile([P, 1], F32, name="warm")
+        warm_out = keep.tile([P, 1], F32, name="warm_out")
+        raw = [keep.tile([P, 2, T], F32, name=f"raw{n}") for n in range(2 * PASSES)]
+        pairs = keep.tile([P, 2 * PASSES * T * 2], BF16, name="pairs", align_bytes=64)
+        slots = [keep.tile([P, E * C, 4], BF16, name=f"slots{s}", align_bytes=64) for s in range(PASSES)]
+        x_codes = [keep.tile([P, E * C], U32, name=f"x_codes{s}", align_bytes=64) for s in range(PASSES)]
+        x_scales = [keep.tile([P, E * C], U8, name=f"x_scales{s}", align_bytes=64) for s in range(PASSES)]
+        out_t = [keep.tile([P, T], F32, name=f"out_t{b}") for b in range(NB)]
+
+        nc.vector.memset(w1_planes[:].rearrange("p a i -> p (a i)").bitcast(I32), 0)
+        nc.gpsimd.memset(w2_planes[:].rearrange("p a i -> p (a i)").bitcast(I32), 0)
+        nc.vector.memset(warm[:], 0.0)
+        nc.scalar.activation(warm_out[:], warm[:], GELU)
+
+        x_rows = xT.rearrange("(s p u j) t -> s u p (j t)", s=PASSES, p=P, u=2)
+        w1_src = w1_words.bitcast(I32).rearrange("e s p b -> e p s b")
+
+        def load_x(n):
+            nc.sync.dma_start(raw[n][:].rearrange("p j t -> p (j t)"), x_rows[n // 2, n % 2])
+
+        def load_w1(e):
+            nc.sync.dma_start(w1_t[e][:].bitcast(I32), w1_src[e])
+
+        w1_sc = w1_scales.bitcast(I32).rearrange("e s (a r) i -> r a (e s) i", r=4)
+        w2_sc = w2_scales.bitcast(I32).rearrange("e s (a r) i -> r a (e s) i", r=4)
+
+        load_x(0)
+        nc.sync.dma_start(offsets[:], offs)
+        load_x(1)
+        for r in range(4):
+            nc.scalar.dma_start(w1_planes[r:P:32].bitcast(I32), w1_sc[r])
+        for n in (2, 3):
+            load_x(n)
+        load_w1(SHARED)
+        load_x(4)
+        load_w1(0)
+        load_x(5)
+        nc.sync.dma_start(w2_t[:].bitcast(I32), w2_words.bitcast(I32).rearrange("e a p b -> p (e a) b"))
+        load_w1(1)
+        nc.sync.dma_start(gate_t[:], gate.rearrange("(b p) j -> p b j", p=P))
+        load_w1(2)
+        load_w1(3)
+
+        for r in range(4):
+            nc.gpsimd.dma_start(w2_planes[r:P:32].bitcast(I32), w2_sc[r])
+        make_identity(nc, ident[:])
+
+        def block(n):
+            return (2 * PASSES - 1 - n) * T
+
+        def cast(n, copy):
+            dst = pairs[:, 2 * block(n) : 2 * (block(n) + T)].rearrange("p (t j) -> p t j", j=2)
+            copy(dst, raw[n][:].rearrange("p j t -> p t j"))
+
+        def gather(n, lo, hi):
+            width = T if n == 0 else 2 * T
+            window = pairs[:, 2 * block(n) : 2 * (block(n) + width)].bitcast(U32)
+            dst = slots[n // 2][:].bitcast(U32)[:, lo:hi, n % 2]
+            nc.vector.tensor_copy(dst, window.indirect(offsets[:, lo // 16 : hi // 16]))
+
+        def quantize_x(s, lo, hi):
+            nc.vector.quantize_mx(
+                out=x_codes[s][:, lo:hi].bitcast(FP8X4),
+                scales=x_scales[s][:, lo:hi],
+                in_=slots[s][:, lo:hi, :].rearrange("p a d -> p (a d)"),
+            )
+
+        acc = {}
+
+        def layer1(c, s):
+            cols = slice(c * C, (c + 1) * C)
+            for i, e in enumerate((c, SHARED)):
+                nc.tensor.matmul_mx(
+                    out=acc[c][i][:],
+                    lhsT=x_codes[s][:, cols].bitcast(FP8X4),
+                    lhsT_scale=x_scales[s][:, cols],
+                    rhs=w1_t[e][:, s, :].bitcast(FP4X4),
+                    rhs_scale=w1_planes[:, e * PASSES + s, :],
+                    start=(s == 0),
+                    stop=(s == PASSES - 1),
+                )
+
+        def open_l1(c):
+            acc_r = ps_l1.tile([P, H], F32, name="acc_r")
+            acc_s = ps_l1.tile([P, H], F32, name="acc_s")
+            acc[c] = (acc_r, acc_s)
+
+        h_act = {}
+
+        def activate(c):
+            h_r = work.tile([P, H], BF16, name="h_r", align_bytes=64)
+            h_s = work.tile([P, H], BF16, name="h_s", align_bytes=64)
+            h_act[c] = (h_r, h_s)
+            nc.scalar.activation(h_r[:], acc[c][0][:], GELU)
+            nc.scalar.activation(h_s[:], acc[c][1][:], GELU)
+
+        h_rows = {}
+
+        def turn(c):
+            turned = ps_t.tile([P, 4, C], F32, name="turned")
+            for i in range(2):
+                words = h_act[c][i][:].bitcast(F32)
+                for u in range(2):
+                    nc.tensor.transpose(turned[:, 2 * i + u, :], words[:, u : H // 2 : 2], ident[:])
+            grouped = work.tile([P, 2, C, 4], BF16, name="grouped", align_bytes=64)
+            h_rows[c] = grouped
+            nc.scalar.copy(grouped[:].bitcast(F32), turned[:].rearrange("p (i u) r -> p i r u", i=2))
+
+        h_q = {}
+
+        def quantize_h(c):
+            h_codes = work.tile([P, 2 * C], U32, name="h_codes", align_bytes=64)
+            h_scales = work.tile([P, 2 * C], U8, name="h_scales", align_bytes=64)
+            h_q[c] = (h_codes, h_scales)
+            nc.vector.quantize_mx(
+                out=h_codes[:].bitcast(FP8X4),
+                scales=h_scales[:],
+                in_=h_rows[c][:].rearrange("p i r d -> p (i r d)"),
+            )
+
+        y = {}
+
+        def layer2(c):
+            y_r = ps_y.tile([P, NB, C], F32, name="y_r")
+            y_s = ps_y.tile([P, NB, C], F32, name="y_s")
+            y[c] = (y_r, y_s)
+            for i, e in enumerate((c, SHARED)):
+                for b in range(NB):
+                    nc.tensor.matmul_mx(
+                        out=y[c][i][:, b, :],
+                        lhsT=w2_t[:, e, 2 * P * b : 2 * P * (b + 1)].bitcast(FP4X4),
+                        lhsT_scale=w2_planes[:, e, P * b : P * (b + 1)],
+                        rhs=h_q[c][0][:, i * C : (i + 1) * C].bitcast(FP8X4),
+                        rhs_scale=h_q[c][1][:, i * C : (i + 1) * C],
+                        start=True,
+                        stop=True,
+                    )
+
+        summed = {}
+
+        def combine(c):
+            gated = work.tile([P, NB, C], F32, name="gated")
+            total = work.tile([P, NB, C], F32, name="total")
+            summed[c] = total
+            nc.vector.tensor_tensor(gated[:], y[c][0][:], gate_t[:, :, c * C : (c + 1) * C], MULT)
+            nc.vector.tensor_tensor(total[:], y[c][1][:], gated[:], ADD)
+
+        def scatter(c):
+            for b in range(NB):
+                where = offsets[:, c * C // 16 : (c + 1) * C // 16]
+                nc.vector.tensor_copy(out_t[b][:].indirect(where), summed[c][:, b, :])
+                if c == E - 1:
+                    nc.sync.dma_start(out[b * P : (b + 1) * P, :], out_t[b][:])
+
+        vec, act = nc.vector.tensor_copy, nc.scalar.copy
+        cast(0, vec)
+        gather(0, 0, 256)
+        gather(0, 256, 512)
+        for n in range(1, 2 * PASSES):
+            cast(n, act)
+        gather(1, 0, 512)
+        gather(2, 0, 512)
+        quantize_x(0, 0, 512)
+        gather(3, 0, 512)
+        gather(4, 0, 128)
+        quantize_x(1, 0, 512)
+        open_l1(0)
+        layer1(0, 0)
+        layer1(0, 1)
+        gather(5, 0, 128)
+        gather(4, 128, 256)
+        quantize_x(2, 0, 128)
+        layer1(0, 2)
+        activate(0)
+        gather(5, 128, 256)
+        gather(4, 256, 512)
+        quantize_x(2, 128, 256)
+        open_l1(1)
+        layer1(1, 0)
+        layer1(1, 1)
+        gather(5, 256, 512)
+        turn(0)
+        layer1(1, 2)
+        activate(1)
+        quantize_x(2, 256, 512)
+        quantize_h(0)
+        layer2(0)
+        for c in range(E):
+            if c + 1 < E:
+                turn(c + 1)
+            if c + 2 < E:
+                open_l1(c + 2)
+                for s in range(PASSES):
+                    layer1(c + 2, s)
+                activate(c + 2)
+            combine(c)
+            if c + 1 < E:
+                quantize_h(c + 1)
+                layer2(c + 1)
+            scatter(c)

@@ -31,7 +31,7 @@ def tile_moe_shr_mlp_gelu_kernel(
     with ExitStack() as ctx:
         keep = ctx.enter_context(tc.tile_pool(name="keep", bufs=1))
         work = ctx.enter_context(tc.tile_pool(name="work", bufs=2))
-        ps_l1 = ctx.enter_context(tc.psum_pool(name="ps_l1", bufs=2))
+        ps_l1 = ctx.enter_context(tc.psum_pool(name="ps_l1", bufs=4))
         ps_t = ctx.enter_context(tc.psum_pool(name="ps_t", bufs=2))
         ps_y = ctx.enter_context(tc.psum_pool(name="ps_y", bufs=1))
 
@@ -46,6 +46,7 @@ def tile_moe_shr_mlp_gelu_kernel(
         warm_out = keep.tile([P, 1], F32, name="warm_out")
         raw = [keep.tile([P, 2, T], F32, name=f"raw{n}") for n in range(2 * PASSES)]
         pairs = keep.tile([P, 2 * PASSES * T * 2], BF16, name="pairs", align_bytes=64)
+        planes = [keep.tile([P, 2, E * C, 2], BF16, name=f"planes{s}", align_bytes=64) for s in range(PASSES)]
         slots = [keep.tile([P, E * C, 4], BF16, name=f"slots{s}", align_bytes=64) for s in range(PASSES)]
         x_codes = [keep.tile([P, E * C], U32, name=f"x_codes{s}", align_bytes=64) for s in range(PASSES)]
         x_scales = [keep.tile([P, E * C], U8, name=f"x_scales{s}", align_bytes=64) for s in range(PASSES)]
@@ -71,20 +72,20 @@ def tile_moe_shr_mlp_gelu_kernel(
         load_x(0)
         nc.sync.dma_start(offsets[:], offs)
         load_x(1)
-        for r in range(4):
-            nc.scalar.dma_start(w1_planes[r:P:32].bitcast(I32), w1_sc[r])
         for n in (2, 3):
             load_x(n)
         load_w1(SHARED)
         load_x(4)
         load_w1(0)
         load_x(5)
-        nc.sync.dma_start(w2_t[:].bitcast(I32), w2_words.bitcast(I32).rearrange("e a p b -> p (e a) b"))
         load_w1(1)
+        nc.sync.dma_start(w2_t[:].bitcast(I32), w2_words.bitcast(I32).rearrange("e a p b -> p (e a) b"))
         nc.sync.dma_start(gate_t[:], gate.rearrange("(b p) j -> p b j", p=P))
         load_w1(2)
         load_w1(3)
 
+        for r in range(4):
+            nc.gpsimd.dma_start(w1_planes[r:P:32].bitcast(I32), w1_sc[r])
         for r in range(4):
             nc.gpsimd.dma_start(w2_planes[r:P:32].bitcast(I32), w2_sc[r])
         make_identity(nc, ident[:])
@@ -99,8 +100,12 @@ def tile_moe_shr_mlp_gelu_kernel(
         def gather(n, lo, hi):
             width = T if n == 0 else 2 * T
             window = pairs[:, 2 * block(n) : 2 * (block(n) + width)].bitcast(U32)
-            dst = slots[n // 2][:].bitcast(U32)[:, lo:hi, n % 2]
+            dst = planes[n // 2][:, n % 2, lo:hi, :].rearrange("p a e -> p (a e)").bitcast(U32)
             nc.vector.tensor_copy(dst, window.indirect(offsets[:, lo // 16 : hi // 16]))
+
+        def interleave(s, lo, hi, copy):
+            src = planes[s][:, :, lo:hi, :].bitcast(F32)[:, :, :, 0].rearrange("p u a -> p a u")
+            copy(slots[s][:, lo:hi, :].bitcast(F32), src)
 
         def quantize_x(s, lo, hi):
             nc.vector.quantize_mx(
@@ -111,134 +116,175 @@ def tile_moe_shr_mlp_gelu_kernel(
 
         acc = {}
 
-        def layer1(c, s):
+        def layer1(c, i, s):
+            if s == 0:
+                tile = ps_l1.tile([P, H], F32, name="acc")
+                acc[c, i] = tile
+            e = (c, SHARED)[i]
             cols = slice(c * C, (c + 1) * C)
-            for i, e in enumerate((c, SHARED)):
-                nc.tensor.matmul_mx(
-                    out=acc[c][i][:],
-                    lhsT=x_codes[s][:, cols].bitcast(FP8X4),
-                    lhsT_scale=x_scales[s][:, cols],
-                    rhs=w1_t[e][:, s, :].bitcast(FP4X4),
-                    rhs_scale=w1_planes[:, e * PASSES + s, :],
-                    start=(s == 0),
-                    stop=(s == PASSES - 1),
-                )
-
-        def open_l1(c):
-            acc_r = ps_l1.tile([P, H], F32, name="acc_r")
-            acc_s = ps_l1.tile([P, H], F32, name="acc_s")
-            acc[c] = (acc_r, acc_s)
+            nc.tensor.matmul_mx(
+                out=acc[c, i][:],
+                lhsT=x_codes[s][:, cols].bitcast(FP8X4),
+                lhsT_scale=x_scales[s][:, cols],
+                rhs=w1_t[e][:, s, :].bitcast(FP4X4),
+                rhs_scale=w1_planes[:, e * PASSES + s, :],
+                start=(s == 0),
+                stop=(s == PASSES - 1),
+            )
 
         h_act = {}
 
-        def activate(c):
-            h_r = work.tile([P, H], BF16, name="h_r", align_bytes=64)
-            h_s = work.tile([P, H], BF16, name="h_s", align_bytes=64)
-            h_act[c] = (h_r, h_s)
-            nc.scalar.activation(h_r[:], acc[c][0][:], GELU)
-            nc.scalar.activation(h_s[:], acc[c][1][:], GELU)
+        def activate(c, i):
+            h = work.tile([P, H], BF16, name=f"h{i}", align_bytes=64)
+            h_act[c, i] = h
+            nc.scalar.activation(h[:], acc[c, i][:], GELU)
 
-        h_rows = {}
+        h_rows, h_q, turned = {}, {}, {}
 
-        def turn(c):
-            turned = ps_t.tile([P, 4, C], F32, name="turned")
-            for i in range(2):
-                words = h_act[c][i][:].bitcast(F32)
+        def turn(c, halves):
+            bank = ps_t.tile([P, 4, C], F32, name="bank")
+            for i in halves:
+                turned[c, i] = bank
+                words = h_act[c, i][:].bitcast(F32)
                 for u in range(2):
-                    nc.tensor.transpose(turned[:, 2 * i + u, :], words[:, u : H // 2 : 2], ident[:])
-            grouped = work.tile([P, 2, C, 4], BF16, name="grouped", align_bytes=64)
-            h_rows[c] = grouped
-            nc.scalar.copy(grouped[:].bitcast(F32), turned[:].rearrange("p (i u) r -> p i r u", i=2))
+                    nc.tensor.transpose(bank[:, 2 * i + u, :], words[:, u : H // 2 : 2], ident[:])
 
-        h_q = {}
+        def group_h(c, halves, copy):
+            if c not in h_rows:
+                rows = work.tile([P, 2, C, 4], BF16, name="rows", align_bytes=64)
+                h_rows[c] = rows
+            lo, hi = halves[0], halves[-1] + 1
+            src = turned[c, lo][:, 2 * lo : 2 * hi, :].rearrange("p (i u) r -> p i r u", u=2)
+            copy(h_rows[c][:, lo:hi].bitcast(F32), src)
 
-        def quantize_h(c):
-            h_codes = work.tile([P, 2 * C], U32, name="h_codes", align_bytes=64)
-            h_scales = work.tile([P, 2 * C], U8, name="h_scales", align_bytes=64)
-            h_q[c] = (h_codes, h_scales)
+        def quantize_h(c, halves):
+            if c not in h_q:
+                h_codes = work.tile([P, 2 * C], U32, name="h_codes", align_bytes=64)
+                h_scales = work.tile([P, 2 * C], U8, name="h_scales", align_bytes=64)
+                h_q[c] = (h_codes, h_scales)
+            lo, hi = halves[0], halves[-1] + 1
             nc.vector.quantize_mx(
-                out=h_codes[:].bitcast(FP8X4),
-                scales=h_scales[:],
-                in_=h_rows[c][:].rearrange("p i r d -> p (i r d)"),
+                out=h_q[c][0][:, lo * C : hi * C].bitcast(FP8X4),
+                scales=h_q[c][1][:, lo * C : hi * C],
+                in_=h_rows[c][:, lo:hi].rearrange("p i r d -> p (i r d)"),
             )
 
         y = {}
 
-        def layer2(c):
-            y_r = ps_y.tile([P, NB, C], F32, name="y_r")
-            y_s = ps_y.tile([P, NB, C], F32, name="y_s")
-            y[c] = (y_r, y_s)
-            for i, e in enumerate((c, SHARED)):
-                for b in range(NB):
-                    nc.tensor.matmul_mx(
-                        out=y[c][i][:, b, :],
-                        lhsT=w2_t[:, e, 2 * P * b : 2 * P * (b + 1)].bitcast(FP4X4),
-                        lhsT_scale=w2_planes[:, e, P * b : P * (b + 1)],
-                        rhs=h_q[c][0][:, i * C : (i + 1) * C].bitcast(FP8X4),
-                        rhs_scale=h_q[c][1][:, i * C : (i + 1) * C],
-                        start=True,
-                        stop=True,
-                    )
+        def layer2(c, i):
+            y_i = ps_y.tile([P, NB, C], F32, name=f"y{i}")
+            y[c, i] = y_i
+            e = (c, SHARED)[i]
+            for b in range(NB):
+                nc.tensor.matmul_mx(
+                    out=y_i[:, b, :],
+                    lhsT=w2_t[:, e, 2 * P * b : 2 * P * (b + 1)].bitcast(FP4X4),
+                    lhsT_scale=w2_planes[:, e, P * b : P * (b + 1)],
+                    rhs=h_q[c][0][:, i * C : (i + 1) * C].bitcast(FP8X4),
+                    rhs_scale=h_q[c][1][:, i * C : (i + 1) * C],
+                    start=True,
+                    stop=True,
+                )
 
-        summed = {}
+        gated, summed = {}, {}
 
-        def combine(c):
-            gated = work.tile([P, NB, C], F32, name="gated")
+        def gate_y(c):
+            gated_c = work.tile([P, NB, C], F32, name="gated_c")
+            gated[c] = gated_c
+            nc.vector.tensor_tensor(gated_c[:], y[c, 0][:], gate_t[:, :, c * C : (c + 1) * C], MULT)
+
+        def add_shared(c):
             total = work.tile([P, NB, C], F32, name="total")
             summed[c] = total
-            nc.vector.tensor_tensor(gated[:], y[c][0][:], gate_t[:, :, c * C : (c + 1) * C], MULT)
-            nc.vector.tensor_tensor(total[:], y[c][1][:], gated[:], ADD)
+            nc.vector.tensor_tensor(total[:], y[c, 1][:], gated[c][:], ADD)
 
-        def scatter(c):
-            for b in range(NB):
+        def scatter(c, blocks):
+            for b in blocks:
                 where = offsets[:, c * C // 16 : (c + 1) * C // 16]
                 nc.vector.tensor_copy(out_t[b][:].indirect(where), summed[c][:, b, :])
                 if c == E - 1:
                     nc.sync.dma_start(out[b * P : (b + 1) * P, :], out_t[b][:])
 
         vec, act = nc.vector.tensor_copy, nc.scalar.copy
+        both = (0, 1)
+
         cast(0, vec)
         gather(0, 0, 256)
         gather(0, 256, 512)
-        for n in range(1, 2 * PASSES):
-            cast(n, act)
+        cast(1, act)
         gather(1, 0, 512)
+        cast(2, act)
+        cast(3, act)
+        interleave(0, 0, 512, act)
         gather(2, 0, 512)
-        quantize_x(0, 0, 512)
         gather(3, 0, 512)
+        quantize_x(0, 0, 512)
+        for i in both:
+            layer1(0, i, 0)
+        cast(4, act)
         gather(4, 0, 128)
+        interleave(1, 0, 512, vec)
+        cast(5, act)
         quantize_x(1, 0, 512)
-        open_l1(0)
-        layer1(0, 0)
-        layer1(0, 1)
+        for i in both:
+            layer1(0, i, 1)
         gather(5, 0, 128)
         gather(4, 128, 256)
-        quantize_x(2, 0, 128)
-        layer1(0, 2)
-        activate(0)
+        interleave(2, 0, 128, vec)
         gather(5, 128, 256)
+        quantize_x(2, 0, 128)
+        for i in both:
+            layer1(1, i, 0)
+        for i in both:
+            layer1(0, i, 2)
+            activate(0, i)
+        interleave(2, 128, 256, vec)
         gather(4, 256, 512)
         quantize_x(2, 128, 256)
-        open_l1(1)
-        layer1(1, 0)
-        layer1(1, 1)
+        for i in both:
+            layer1(1, i, 1)
+        turn(0, (0,))
+        for i in both:
+            layer1(1, i, 2)
+        turn(0, (1,))
+        group_h(0, (0,), vec)
+        group_h(0, (1,), act)
         gather(5, 256, 512)
-        turn(0)
-        layer1(1, 2)
-        activate(1)
+        quantize_h(0, (0,))
+        interleave(2, 256, 512, vec)
+        layer2(0, 0)
+        for i in both:
+            activate(1, i)
+        quantize_h(0, (1,))
+        layer2(0, 1)
         quantize_x(2, 256, 512)
-        quantize_h(0)
-        layer2(0)
-        for c in range(E):
+        gate_y(0)
+        turn(1, both)
+        group_h(1, both, act)
+        for i in both:
+            for s in range(PASSES):
+                layer1(2, i, s)
+            activate(2, i)
+        add_shared(0)
+        scatter(0, (0, 1))
+        quantize_h(1, both)
+        layer2(1, 0)
+        layer2(1, 1)
+        scatter(0, (2,))
+        turn(2, both)
+        group_h(2, both, act)
+        for i in both:
+            for s in range(PASSES):
+                layer1(3, i, s)
+            activate(3, i)
+        for c in (1, 2, 3):
+            gate_y(c)
+            add_shared(c)
             if c + 1 < E:
-                turn(c + 1)
+                quantize_h(c + 1, both)
+                layer2(c + 1, 0)
+                layer2(c + 1, 1)
             if c + 2 < E:
-                open_l1(c + 2)
-                for s in range(PASSES):
-                    layer1(c + 2, s)
-                activate(c + 2)
-            combine(c)
-            if c + 1 < E:
-                quantize_h(c + 1)
-                layer2(c + 1)
-            scatter(c)
+                turn(c + 2, both)
+                group_h(c + 2, both, act)
+            scatter(c, range(NB))

@@ -10,6 +10,7 @@ P = 128
 SHARED = E
 PASSES = K // 512
 NB = N // P
+ON_GPSIMD = (1, 2, 3,)
 
 F32 = mybir.dt.float32
 BF16 = mybir.dt.bfloat16
@@ -39,12 +40,14 @@ def tile_moe_shr_mlp_gelu_kernel(
         w1_planes = keep.tile([P, (E + 1) * PASSES, H], U8, name="w1_planes", align_bytes=64)
         w2_planes = keep.tile([P, E + 1, N], U8, name="w2_planes", align_bytes=64)
         w2_t = keep.tile([P, E + 1, 2 * N], U8, name="w2_t", align_bytes=64)
-        w1_t = [keep.tile([P, PASSES, 2 * H], U8, name=f"w1_t{e}", align_bytes=64) for e in range(E + 1)]
+        w1_t = keep.tile([P, E + 1, PASSES, 2 * H], U8, name="w1_t", align_bytes=64)
         gate_t = keep.tile([P, NB, E * C], F32, name="gate_t")
         ident = keep.tile([P, P], F32, name="ident")
         warm = keep.tile([P, 1], F32, name="warm")
         warm_out = keep.tile([P, 1], F32, name="warm_out")
-        raw = [keep.tile([P, 2, T], F32, name=f"raw{n}") for n in range(2 * PASSES)]
+        raw_0 = keep.tile([P, 2, 2, T], F32, name="raw_0")
+        raw_1 = keep.tile([P, 4, 2, T], F32, name="raw_1")
+        raw = [raw_0[:, n] for n in range(2)] + [raw_1[:, n] for n in range(4)]
         pairs = keep.tile([P, 2 * PASSES * T * 2], BF16, name="pairs", align_bytes=64)
         planes = [keep.tile([P, 2, E * C, 2], BF16, name=f"planes{s}", align_bytes=64) for s in range(PASSES)]
         slots = [keep.tile([P, E * C, 4], BF16, name=f"slots{s}", align_bytes=64) for s in range(PASSES)]
@@ -52,7 +55,12 @@ def tile_moe_shr_mlp_gelu_kernel(
         x_scales = [keep.tile([P, E * C], U8, name=f"x_scales{s}", align_bytes=64) for s in range(PASSES)]
         out_t = [keep.tile([P, T], F32, name=f"out_t{b}") for b in range(NB)]
 
-        nc.vector.memset(w1_planes[:].rearrange("p a i -> p (a i)").bitcast(I32), 0)
+        nc.vector.memset(w1_planes[:, 0:10, :].rearrange("p a i -> p (a i)").bitcast(I32), 0)
+        nc.gpsimd.memset(w1_planes[:, 10:15, :].rearrange("p a i -> p (a i)").bitcast(I32), 0)
+        nc.vector.memset(raw_1[:, :, 0, 0:1], 0.0)
+        nc.vector.memset(w1_t[:].bitcast(I32)[:, :, 0, 0:1], 0)
+        nc.vector.memset(w2_t[:].bitcast(I32)[:, :, 0:1], 0)
+        nc.vector.memset(gate_t[:, :, 0:1], 0.0)
         nc.gpsimd.memset(w2_planes[:].rearrange("p a i -> p (a i)").bitcast(I32), 0)
         nc.vector.memset(warm[:], 0.0)
         nc.scalar.activation(warm_out[:], warm[:], GELU)
@@ -61,10 +69,10 @@ def tile_moe_shr_mlp_gelu_kernel(
         w1_src = w1_words.bitcast(I32).rearrange("e s p b -> e p s b")
 
         def load_x(n):
-            nc.sync.dma_start(raw[n][:].rearrange("p j t -> p (j t)"), x_rows[n // 2, n % 2])
+            nc.sync.dma_start(raw[n].rearrange("p j t -> p (j t)"), x_rows[n // 2, n % 2])
 
         def load_w1(e):
-            nc.sync.dma_start(w1_t[e][:].bitcast(I32), w1_src[e])
+            nc.sync.dma_start(w1_t[:, e].bitcast(I32), w1_src[e])
 
         w1_sc = w1_scales.bitcast(I32).rearrange("e s (a r) i -> r a (e s) i", r=4)
         w2_sc = w2_scales.bitcast(I32).rearrange("e s (a r) i -> r a (e s) i", r=4)
@@ -72,6 +80,8 @@ def tile_moe_shr_mlp_gelu_kernel(
         load_x(0)
         nc.sync.dma_start(offsets[:], offs)
         load_x(1)
+        for r in range(4):
+            nc.sync.dma_start(w1_planes[r:P:32].bitcast(I32), w1_sc[r])
         for n in (2, 3):
             load_x(n)
         load_w1(SHARED)
@@ -85,8 +95,6 @@ def tile_moe_shr_mlp_gelu_kernel(
         load_w1(3)
 
         for r in range(4):
-            nc.gpsimd.dma_start(w1_planes[r:P:32].bitcast(I32), w1_sc[r])
-        for r in range(4):
             nc.gpsimd.dma_start(w2_planes[r:P:32].bitcast(I32), w2_sc[r])
         make_identity(nc, ident[:])
 
@@ -95,7 +103,7 @@ def tile_moe_shr_mlp_gelu_kernel(
 
         def cast(n, copy):
             dst = pairs[:, 2 * block(n) : 2 * (block(n) + T)].rearrange("p (t j) -> p t j", j=2)
-            copy(dst, raw[n][:].rearrange("p j t -> p t j"))
+            copy(dst, raw[n].rearrange("p j t -> p t j"))
 
         def gather(n, lo, hi):
             width = T if n == 0 else 2 * T
@@ -126,7 +134,7 @@ def tile_moe_shr_mlp_gelu_kernel(
                 out=acc[c, i][:],
                 lhsT=x_codes[s][:, cols].bitcast(FP8X4),
                 lhsT_scale=x_scales[s][:, cols],
-                rhs=w1_t[e][:, s, :].bitcast(FP4X4),
+                rhs=w1_t[:, e, s, :].bitcast(FP4X4),
                 rhs_scale=w1_planes[:, e * PASSES + s, :],
                 start=(s == 0),
                 stop=(s == PASSES - 1),
@@ -191,7 +199,13 @@ def tile_moe_shr_mlp_gelu_kernel(
         def gate_y(c):
             gated_c = work.tile([P, NB, C], F32, name="gated_c")
             gated[c] = gated_c
-            nc.vector.tensor_tensor(gated_c[:], y[c, 0][:], gate_t[:, :, c * C : (c + 1) * C], MULT)
+            gate_c = gate_t[:, :, c * C : (c + 1) * C]
+            if c in ON_GPSIMD:
+                y_rows = work.tile([P, NB, C], F32, name="y_rows")
+                nc.scalar.copy(y_rows[:], y[c, 0][:])
+                nc.gpsimd.tensor_tensor(gated_c[:], y_rows[:], gate_c, MULT)
+            else:
+                nc.vector.tensor_tensor(gated_c[:], y[c, 0][:], gate_c, MULT)
 
         def add_shared(c):
             total = work.tile([P, NB, C], F32, name="total")
@@ -277,13 +291,15 @@ def tile_moe_shr_mlp_gelu_kernel(
             for s in range(PASSES):
                 layer1(3, i, s)
             activate(3, i)
+        gate_y(1)
         for c in (1, 2, 3):
-            gate_y(c)
-            add_shared(c)
             if c + 1 < E:
                 quantize_h(c + 1, both)
+            add_shared(c)
+            if c + 1 < E:
                 layer2(c + 1, 0)
                 layer2(c + 1, 1)
+                gate_y(c + 1)
             if c + 2 < E:
                 turn(c + 2, both)
                 group_h(c + 2, both, act)

@@ -45,9 +45,9 @@ def tile_moe_shr_mlp_gelu_kernel(
         ident = keep.tile([P, P], F32, name="ident")
         warm = keep.tile([P, 1], F32, name="warm")
         warm_out = keep.tile([P, 1], F32, name="warm_out")
-        raw_0 = keep.tile([P, 2, 2, T], F32, name="raw_0")
-        raw_1 = keep.tile([P, 4, 2, T], F32, name="raw_1")
-        raw = [raw_0[:, n] for n in range(2)] + [raw_1[:, n] for n in range(4)]
+        raw_0 = keep.tile([P, 3, 2, T], F32, name="raw_0")
+        raw_1 = keep.tile([P, 3, 2, T], F32, name="raw_1")
+        raw = [raw_0[:, n] for n in range(3)] + [raw_1[:, n] for n in range(3)]
         pairs = keep.tile([P, 2 * PASSES * T * 2], BF16, name="pairs", align_bytes=64)
         planes = [keep.tile([P, 2, E * C, 2], BF16, name=f"planes{s}", align_bytes=64) for s in range(PASSES)]
         slots = [keep.tile([P, E * C, 4], BF16, name=f"slots{s}", align_bytes=64) for s in range(PASSES)]
@@ -62,6 +62,7 @@ def tile_moe_shr_mlp_gelu_kernel(
         nc.vector.memset(w2_t[:].bitcast(I32)[:, :, 0:1], 0)
         nc.vector.memset(gate_t[:, :, 0:1], 0.0)
         nc.gpsimd.memset(w2_planes[:].rearrange("p a i -> p (a i)").bitcast(I32), 0)
+        make_identity(nc, ident[:])
         nc.vector.memset(warm[:], 0.0)
         nc.scalar.activation(warm_out[:], warm[:], GELU)
 
@@ -80,14 +81,14 @@ def tile_moe_shr_mlp_gelu_kernel(
         load_x(0)
         nc.sync.dma_start(offsets[:], offs)
         load_x(1)
+        load_x(2)
         for r in range(4):
             nc.sync.dma_start(w1_planes[r:P:32].bitcast(I32), w1_sc[r])
-        for n in (2, 3):
-            load_x(n)
-        load_w1(SHARED)
+        load_x(3)
         load_x(4)
-        load_w1(0)
+        load_w1(SHARED)
         load_x(5)
+        load_w1(0)
         load_w1(1)
         nc.sync.dma_start(w2_t[:].bitcast(I32), w2_words.bitcast(I32).rearrange("e a p b -> p (e a) b"))
         nc.sync.dma_start(gate_t[:], gate.rearrange("(b p) j -> p b j", p=P))
@@ -96,7 +97,6 @@ def tile_moe_shr_mlp_gelu_kernel(
 
         for r in range(4):
             nc.gpsimd.dma_start(w2_planes[r:P:32].bitcast(I32), w2_sc[r])
-        make_identity(nc, ident[:])
 
         def block(n):
             return (2 * PASSES - 1 - n) * T

from contextlib import ExitStack

import concourse.mybir as mybir
from concourse.masks import make_identity

FLOPS = 2013265920

K, T, E, C, H, N = 1536, 512, 4, 128, 512, 384
P = 128
SHARED = E
PASSES = K // 512
NB = N // P
ON_GPSIMD = (1, 2, 3,)

F32 = mybir.dt.float32
BF16 = mybir.dt.bfloat16
I32 = mybir.dt.int32
U32 = mybir.dt.uint32
U16 = mybir.dt.uint16
U8 = mybir.dt.uint8
FP8X4 = mybir.dt.float8_e4m3fn_x4
FP4X4 = mybir.dt.float4_e2m1fn_x4
ADD = mybir.AluOpType.add
MULT = mybir.AluOpType.mult
GELU = mybir.ActivationFunctionType.Gelu_apprx_tanh


def tile_moe_shr_mlp_gelu_kernel(
    tc, xT, w1_words, w1_scales, w2_words, w2_scales, gate, offs, out
):
    nc = tc.nc
    with ExitStack() as ctx:
        keep = ctx.enter_context(tc.tile_pool(name="keep", bufs=1))
        work = ctx.enter_context(tc.tile_pool(name="work", bufs=2))
        ps_l1 = ctx.enter_context(tc.psum_pool(name="ps_l1", bufs=4))
        ps_t = ctx.enter_context(tc.psum_pool(name="ps_t", bufs=2))
        ps_y = ctx.enter_context(tc.psum_pool(name="ps_y", bufs=1))

        offsets = keep.tile([P, E * C // 16], U16, name="offsets")
        w1_planes = keep.tile([P, (E + 1) * PASSES, H], U8, name="w1_planes", align_bytes=64)
        w2_planes = keep.tile([P, E + 1, N], U8, name="w2_planes", align_bytes=64)
        w2_t = keep.tile([P, E + 1, 2 * N], U8, name="w2_t", align_bytes=64)
        w1_t = keep.tile([P, E + 1, PASSES, 2 * H], U8, name="w1_t", align_bytes=64)
        gate_t = keep.tile([P, NB, E * C], F32, name="gate_t")
        ident = keep.tile([P, P], F32, name="ident")
        warm = keep.tile([P, 1], F32, name="warm")
        warm_out = keep.tile([P, 1], F32, name="warm_out")
        raw_0 = keep.tile([P, 3, 2, T], F32, name="raw_0")
        raw_1 = keep.tile([P, 3, 2, T], F32, name="raw_1")
        raw = [raw_0[:, n] for n in range(3)] + [raw_1[:, n] for n in range(3)]
        pairs = keep.tile([P, 2 * PASSES * T * 2], BF16, name="pairs", align_bytes=64)
        planes = [keep.tile([P, 2, E * C, 2], BF16, name=f"planes{s}", align_bytes=64) for s in range(PASSES)]
        slots = [keep.tile([P, E * C, 4], BF16, name=f"slots{s}", align_bytes=64) for s in range(PASSES)]
        x_codes = [keep.tile([P, E * C], U32, name=f"x_codes{s}", align_bytes=64) for s in range(PASSES)]
        x_scales = [keep.tile([P, E * C], U8, name=f"x_scales{s}", align_bytes=64) for s in range(PASSES)]
        out_t = [keep.tile([P, T], F32, name=f"out_t{b}") for b in range(NB)]

        nc.vector.memset(w1_planes[:, 0:10, :].rearrange("p a i -> p (a i)").bitcast(I32), 0)
        nc.gpsimd.memset(w1_planes[:, 10:15, :].rearrange("p a i -> p (a i)").bitcast(I32), 0)
        nc.vector.memset(raw_1[:, :, 0, 0:1], 0.0)
        nc.vector.memset(w1_t[:].bitcast(I32)[:, :, 0, 0:1], 0)
        nc.vector.memset(w2_t[:].bitcast(I32)[:, :, 0:1], 0)
        nc.vector.memset(gate_t[:, :, 0:1], 0.0)
        nc.gpsimd.memset(w2_planes[:].rearrange("p a i -> p (a i)").bitcast(I32), 0)
        make_identity(nc, ident[:])
        nc.vector.memset(warm[:], 0.0)
        nc.scalar.activation(warm_out[:], warm[:], GELU)

        x_rows = xT.rearrange("(s p u j) t -> s u p (j t)", s=PASSES, p=P, u=2)
        w1_src = w1_words.bitcast(I32).rearrange("e s p b -> e p s b")

        def load_x(n):
            nc.sync.dma_start(raw[n].rearrange("p j t -> p (j t)"), x_rows[n // 2, n % 2])

        def load_w1(e):
            nc.sync.dma_start(w1_t[:, e].bitcast(I32), w1_src[e])

        w1_sc = w1_scales.bitcast(I32).rearrange("e s (a r) i -> r a (e s) i", r=4)
        w2_sc = w2_scales.bitcast(I32).rearrange("e s (a r) i -> r a (e s) i", r=4)

        load_x(0)
        nc.sync.dma_start(offsets[:], offs)
        load_x(1)
        load_x(2)
        for r in range(4):
            nc.sync.dma_start(w1_planes[r:P:32].bitcast(I32), w1_sc[r])
        load_x(3)
        load_x(4)
        load_w1(SHARED)
        load_x(5)
        load_w1(0)
        load_w1(1)
        nc.sync.dma_start(w2_t[:].bitcast(I32), w2_words.bitcast(I32).rearrange("e a p b -> p (e a) b"))
        nc.sync.dma_start(gate_t[:], gate.rearrange("(b p) j -> p b j", p=P))
        load_w1(2)
        load_w1(3)

        for r in range(4):
            nc.gpsimd.dma_start(w2_planes[r:P:32].bitcast(I32), w2_sc[r])

        def block(n):
            return (2 * PASSES - 1 - n) * T

        def cast(n, copy):
            dst = pairs[:, 2 * block(n) : 2 * (block(n) + T)].rearrange("p (t j) -> p t j", j=2)
            copy(dst, raw[n].rearrange("p j t -> p t j"))

        def gather(n, lo, hi):
            width = T if n == 0 else 2 * T
            window = pairs[:, 2 * block(n) : 2 * (block(n) + width)].bitcast(U32)
            dst = planes[n // 2][:, n % 2, lo:hi, :].rearrange("p a e -> p (a e)").bitcast(U32)
            nc.vector.tensor_copy(dst, window.indirect(offsets[:, lo // 16 : hi // 16]))

        def interleave(s, lo, hi, copy):
            src = planes[s][:, :, lo:hi, :].bitcast(F32)[:, :, :, 0].rearrange("p u a -> p a u")
            copy(slots[s][:, lo:hi, :].bitcast(F32), src)

        def quantize_x(s, lo, hi):
            nc.vector.quantize_mx(
                out=x_codes[s][:, lo:hi].bitcast(FP8X4),
                scales=x_scales[s][:, lo:hi],
                in_=slots[s][:, lo:hi, :].rearrange("p a d -> p (a d)"),
            )

        acc = {}

        def layer1(c, i, s):
            if s == 0:
                tile = ps_l1.tile([P, H], F32, name="acc")
                acc[c, i] = tile
            e = (c, SHARED)[i]
            cols = slice(c * C, (c + 1) * C)
            nc.tensor.matmul_mx(
                out=acc[c, i][:],
                lhsT=x_codes[s][:, cols].bitcast(FP8X4),
                lhsT_scale=x_scales[s][:, cols],
                rhs=w1_t[:, e, s, :].bitcast(FP4X4),
                rhs_scale=w1_planes[:, e * PASSES + s, :],
                start=(s == 0),
                stop=(s == PASSES - 1),
            )

        h_act = {}

        def activate(c, i):
            h = work.tile([P, H], BF16, name=f"h{i}", align_bytes=64)
            h_act[c, i] = h
            nc.scalar.activation(h[:], acc[c, i][:], GELU)

        h_rows, h_q, turned = {}, {}, {}

        def turn(c, halves):
            bank = ps_t.tile([P, 4, C], F32, name="bank")
            for i in halves:
                turned[c, i] = bank
                words = h_act[c, i][:].bitcast(F32)
                for u in range(2):
                    nc.tensor.transpose(bank[:, 2 * i + u, :], words[:, u : H // 2 : 2], ident[:])

        def group_h(c, halves, copy):
            if c not in h_rows:
                rows = work.tile([P, 2, C, 4], BF16, name="rows", align_bytes=64)
                h_rows[c] = rows
            lo, hi = halves[0], halves[-1] + 1
            src = turned[c, lo][:, 2 * lo : 2 * hi, :].rearrange("p (i u) r -> p i r u", u=2)
            copy(h_rows[c][:, lo:hi].bitcast(F32), src)

        def quantize_h(c, halves):
            if c not in h_q:
                h_codes = work.tile([P, 2 * C], U32, name="h_codes", align_bytes=64)
                h_scales = work.tile([P, 2 * C], U8, name="h_scales", align_bytes=64)
                h_q[c] = (h_codes, h_scales)
            lo, hi = halves[0], halves[-1] + 1
            nc.vector.quantize_mx(
                out=h_q[c][0][:, lo * C : hi * C].bitcast(FP8X4),
                scales=h_q[c][1][:, lo * C : hi * C],
                in_=h_rows[c][:, lo:hi].rearrange("p i r d -> p (i r d)"),
            )

        y = {}

        def layer2(c, i):
            y_i = ps_y.tile([P, NB, C], F32, name=f"y{i}")
            y[c, i] = y_i
            e = (c, SHARED)[i]
            for b in range(NB):
                nc.tensor.matmul_mx(
                    out=y_i[:, b, :],
                    lhsT=w2_t[:, e, 2 * P * b : 2 * P * (b + 1)].bitcast(FP4X4),
                    lhsT_scale=w2_planes[:, e, P * b : P * (b + 1)],
                    rhs=h_q[c][0][:, i * C : (i + 1) * C].bitcast(FP8X4),
                    rhs_scale=h_q[c][1][:, i * C : (i + 1) * C],
                    start=True,
                    stop=True,
                )

        gated, summed = {}, {}

        def gate_y(c):
            gated_c = work.tile([P, NB, C], F32, name="gated_c")
            gated[c] = gated_c
            gate_c = gate_t[:, :, c * C : (c + 1) * C]
            if c in ON_GPSIMD:
                y_rows = work.tile([P, NB, C], F32, name="y_rows")
                nc.scalar.copy(y_rows[:], y[c, 0][:])
                nc.gpsimd.tensor_tensor(gated_c[:], y_rows[:], gate_c, MULT)
            else:
                nc.vector.tensor_tensor(gated_c[:], y[c, 0][:], gate_c, MULT)

        def add_shared(c):
            total = work.tile([P, NB, C], F32, name="total")
            summed[c] = total
            nc.vector.tensor_tensor(total[:], y[c, 1][:], gated[c][:], ADD)

        def scatter(c, blocks):
            for b in blocks:
                where = offsets[:, c * C // 16 : (c + 1) * C // 16]
                nc.vector.tensor_copy(out_t[b][:].indirect(where), summed[c][:, b, :])
                if c == E - 1:
                    nc.sync.dma_start(out[b * P : (b + 1) * P, :], out_t[b][:])

        vec, act = nc.vector.tensor_copy, nc.scalar.copy
        both = (0, 1)

        cast(0, vec)
        gather(0, 0, 256)
        gather(0, 256, 512)
        cast(1, act)
        gather(1, 0, 512)
        cast(2, act)
        cast(3, act)
        interleave(0, 0, 512, act)
        gather(2, 0, 512)
        gather(3, 0, 512)
        quantize_x(0, 0, 512)
        for i in both:
            layer1(0, i, 0)
        cast(4, act)
        gather(4, 0, 128)
        interleave(1, 0, 512, vec)
        cast(5, act)
        quantize_x(1, 0, 512)
        for i in both:
            layer1(0, i, 1)
        gather(5, 0, 128)
        gather(4, 128, 256)
        interleave(2, 0, 128, vec)
        gather(5, 128, 256)
        quantize_x(2, 0, 128)
        for i in both:
            layer1(1, i, 0)
        for i in both:
            layer1(0, i, 2)
            activate(0, i)
        interleave(2, 128, 256, vec)
        gather(4, 256, 512)
        quantize_x(2, 128, 256)
        for i in both:
            layer1(1, i, 1)
        turn(0, (0,))
        for i in both:
            layer1(1, i, 2)
        turn(0, (1,))
        group_h(0, (0,), vec)
        group_h(0, (1,), act)
        gather(5, 256, 512)
        quantize_h(0, (0,))
        interleave(2, 256, 512, vec)
        layer2(0, 0)
        for i in both:
            activate(1, i)
        quantize_h(0, (1,))
        layer2(0, 1)
        quantize_x(2, 256, 512)
        gate_y(0)
        turn(1, both)
        group_h(1, both, act)
        for i in both:
            for s in range(PASSES):
                layer1(2, i, s)
            activate(2, i)
        add_shared(0)
        scatter(0, (0, 1))
        quantize_h(1, both)
        layer2(1, 0)
        layer2(1, 1)
        scatter(0, (2,))
        turn(2, both)
        group_h(2, both, act)
        for i in both:
            for s in range(PASSES):
                layer1(3, i, s)
            activate(3, i)
        gate_y(1)
        for c in (1, 2, 3):
            if c + 1 < E:
                quantize_h(c + 1, both)
            add_shared(c)
            if c + 1 < E:
                layer2(c + 1, 0)
                layer2(c + 1, 1)
                gate_y(c + 1)
            if c + 2 < E:
                turn(c + 2, both)
                group_h(c + 2, both, act)
            scatter(c, range(NB))
